import numpy as np
import ml_dtypes


def mxq(x, axis, fmt="e4m3"):
    dtype, down = {"e4m3": (ml_dtypes.float8_e4m3fn, 7), "e5m2": (ml_dtypes.float8_e5m2, 14)}[fmt]
    v = np.moveaxis(np.asarray(x, np.float32).astype(ml_dtypes.bfloat16).astype(np.float64), axis, -1)
    blocks = v.reshape(v.shape[:-1] + (-1, 32))
    amax = np.abs(blocks).max(-1, keepdims=True)
    byte = np.maximum(np.where(amax > 0, np.frexp(amax)[1] - 1 + 127, 0) - down, 1)
    scale = np.exp2(byte - 127.0)
    codes = (blocks / scale).astype(np.float32).astype(dtype).astype(np.float64)
    return np.moveaxis((codes * scale).reshape(v.shape), -1, axis)


WIDE = False


def mx_kscale(k):
    if not WIDE:
        return np.ones(k)
    levels = np.array([10, -10, 5, -5, 0])
    if k % 512:
        return np.exp2(np.random.permutation(np.resize(levels, k // 32))).repeat(32)
    a = np.empty((k // 512, 16))
    for p in range(k // 512):
        a[p, :8] = np.random.permutation(np.resize(levels, 8))
        for g in range(8):
            far = levels[np.abs(levels - a[p, g]) >= 10]
            a[p, g + 8] = far[np.random.randint(len(far))]
    return np.exp2(a.ravel()).repeat(32)


def f64(x):
    return np.asarray(x).astype(np.float64)


def striped(idx):
    return np.tile(idx.reshape(-1, 16).T, (8, 1)).astype(np.uint16)


def unstriped(offs):
    return offs[:16].T.reshape(-1).astype(np.int64)


def striped8(idx):
    return np.concatenate([x.reshape(-1, 16).T for x in idx]).astype(np.uint16)


def runs(offs, k):
    lists = np.stack([offs[16 * r : 16 * r + 16].T.reshape(-1) for r in range(8)]).astype(np.int64)
    return lists[np.arange(k) % 512 // 64]


def pack_weight(w):
    k, n = w.shape
    w = f64(np.asarray(w, np.float32).astype(ml_dtypes.bfloat16)).reshape(k // 32, 32, n)
    amax = np.abs(w).max(1)
    byte = np.clip(np.where(amax > 0, np.frexp(amax)[1] - 1 + 127 - 7, 1), 1, 254)
    scaled = (w * np.exp2(127.0 - byte)[:, None, :]).reshape(k, n).astype(np.float32)
    words = np.ascontiguousarray(scaled.reshape(k // 512, 128, 4, n).transpose(0, 1, 3, 2)).astype(ml_dtypes.float8_e4m3fn).view(np.uint8)
    return words, np.ascontiguousarray(byte.astype(np.uint8).reshape(k // 512, 16, n))


def unpack_weight(words, scales):
    g, p, n, _ = words.shape
    vals = np.ascontiguousarray(words).view(ml_dtypes.float8_e4m3fn).astype(np.float64) * np.repeat(np.exp2(scales.astype(np.float64) - 127.0), 8, axis=1)[..., None]
    return vals.transpose(0, 1, 3, 2).reshape(g * 512, n)


E2M1 = np.array([0.0, 0.5, 1.0, 1.5, 2.0, 3.0, 4.0, 6.0, -0.0, -0.5, -1.0, -1.5, -2.0, -3.0, -4.0, -6.0])


def pack_fp4(w):
    k, n = w.shape
    w = f64(np.asarray(w, np.float32).astype(ml_dtypes.bfloat16)).reshape(k // 32, 32, n)
    amax = np.abs(w).max(1)
    mant, ex = np.frexp(amax / 6.0)
    byte = np.clip(np.where(amax > 0, np.where(mant > 0.5, ex, ex - 1) + 127, 1), 1, 254)
    scaled = (w * np.exp2(127.0 - byte)[:, None, :]).reshape(k, n).astype(np.float32)
    c = np.ascontiguousarray(scaled.reshape(k // 512, 128, 4, n).transpose(0, 1, 3, 2)).astype(ml_dtypes.float4_e2m1fn).view(np.uint8) & 0xF
    words = (c[..., 0::2] | (c[..., 1::2] << 4)).reshape(k // 512, 128, 2 * n)
    return np.ascontiguousarray(words), np.ascontiguousarray(byte.astype(np.uint8).reshape(k // 512, 16, n))


def unpack_fp4(words, scales):
    g, _, n = scales.shape
    words = np.ascontiguousarray(words).reshape(g, 128, n, 2)
    nib = np.empty((g, 128, n, 4), np.uint8)
    nib[..., 0::2] = words & 0xF
    nib[..., 1::2] = words >> 4
    vals = E2M1[nib] * np.repeat(np.exp2(scales.astype(np.float64) - 127.0), 8, axis=1)[..., None]
    return vals.transpose(0, 1, 3, 2).reshape(g * 512, n)


def planes(y):
    n, m = y.shape
    v = y.astype(np.float32).astype(ml_dtypes.bfloat16).astype(np.float64).reshape(n // 32, 32, m)
    top = np.abs(v).max(1)
    byte = np.clip(np.where(top > 0, np.frexp(top)[1] - 1 + 127 - 7, 1), 1, 254)
    codes = (v * np.exp2(127.0 - byte)[:, None, :]).reshape(n, m).astype(np.float32).astype(ml_dtypes.float8_e4m3fn).view(np.uint8)
    words = codes.reshape(n // 512, 128, 4, m).transpose(0, 1, 3, 2)
    return np.ascontiguousarray(words), np.ascontiguousarray(byte.astype(np.uint8).reshape(n // 512, 16, m))


K, T, S, N, G, H, W = 512, 1024, 512, 512, 2048, 512, 1024


def setup_inputs():
    n = np.random.standard_normal
    s = mx_kscale(K)[:, None]
    u = mx_kscale(S)
    packed_xT = pack_weight(n((K, T)) * s)
    packed_dT = pack_weight(n((K, G)) / s)
    packed_w1 = pack_fp4(n((H, N)) / np.sqrt(2 * H) / u[:, None])
    packed_w2 = pack_fp4(n((K, N)) / np.sqrt(2 * K) / s)
    return {
        "x_words": packed_xT[0],
        "x_scales": packed_xT[1],
        "d_words": packed_dT[0],
        "d_scales": packed_dT[1],
        "gn": (np.random.uniform(0.5, 1.5, (H, 1)) * u[:, None]).astype(np.float32),
        "w1_words": packed_w1[0],
        "w1_scales": packed_w1[1],
        "w2_words": packed_w2[0],
        "w2_scales": packed_w2[1],
        "offs": striped(np.random.permutation(T)[:S]),
        "k1": striped8(np.random.randint(0, G, (8, H))),
        "n1": striped(np.random.randint(0, S, W)),
        "n2": striped(np.random.permutation(S)),
        "two": striped(np.random.permutation(T)[:S]),
        "n3": striped8(np.stack([np.random.permutation(S) for _ in range(8)])),
        "n4": striped8(np.stack([np.random.permutation(S) for _ in range(8)])),
    }


def reference(x_words, x_scales, d_words, d_scales, gn, w1_words, w1_scales, w2_words, w2_scales, offs, k1, n1, n2, two, n3, n4):
    d_k1 = unpack_weight(d_words, d_scales)[np.arange(K)[:, None], runs(k1, K)]
    xq = unpack_weight(x_words, x_scales)[:, unstriped(offs)]
    h = 0.0625 * (d_k1.T @ xq)
    mb = h[:, unstriped(n1)]
    mx = mb.reshape(H, S, 2).max(axis=2)
    st = h - mx
    z = f64(gn) * (np.maximum(st, st[:, unstriped(n2)]))
    x_two = unpack_weight(x_words, x_scales)[:, unstriped(two)]
    h2 = unpack_fp4(w1_words, w1_scales).T @ mxq(z, 0, "e4m3") + unpack_fp4(w2_words, w2_scales).T @ x_two
    st2 = np.maximum(h2, h2[np.arange(N)[:, None], runs(n3, N)])
    out_0 = st2[np.arange(N)[:, None], runs(n4, N)] - (0.5 * h2)
    return (out_0,) + planes(out_0)

@@ -1,0 +1,375 @@
+from contextlib import ExitStack
+
+import concourse.mybir as mybir
+
+F32 = mybir.dt.float32
+BF16 = mybir.dt.bfloat16
+I32 = mybir.dt.int32
+U32 = mybir.dt.uint32
+U16 = mybir.dt.uint16
+U8 = mybir.dt.uint8
+FP8X4 = mybir.dt.float8_e4m3fn_x4
+FP4X4 = mybir.dt.float4_e2m1fn_x4
+COPY = mybir.ActivationFunctionType.Copy
+MAX = mybir.AluOpType.max
+MULT = mybir.AluOpType.mult
+ADD = mybir.AluOpType.add
+SUB = mybir.AluOpType.subtract
+
+P = 128
+PACK = 4
+S = 512
+T = 1024
+G = 2048
+HALF = S // 2
+SPARE = 16
+Z_CUTS = (0, 256, 512)
+O_CUTS = (0, 256, 512)
+FLOPS = 3 * 2 * 512 * 512 * 512
+
+
+def tile_picked_pqmixghopmhopb_none_po_kernel(
+    tc, x_words, x_scales, d_words, d_scales, gn, w1_words, w1_scales, w2_words, w2_scales,
+    offs, k1, n1, n2, two, n3, n4, out_0, out_1, out_2,
+):
+    nc = tc.nc
+    with ExitStack() as ctx:
+        keep = ctx.enter_context(tc.tile_pool(name="keep", bufs=1))
+        psum = ctx.enter_context(tc.psum_pool(name="psum", bufs=8))
+
+        def sb(name, width, dtype):
+            return keep.tile([P, width], dtype, name=name, align_bytes=64)
+
+        def load_list(name, src):
+            t = keep.tile([P, src.shape[1]], U16, name=name)
+            nc.sync.dma_start(t[:], src)
+            return t
+
+        def zero(ap):
+            nc.vector.memset(ap.bitcast(I32), 0)
+
+        def gather(engine, out, window, offsets):
+            if engine == "S":
+                nc.scalar.activation(out, window[:].indirect(offsets), COPY)
+            else:
+                nc.vector.tensor_copy(out, window[:].indirect(offsets))
+
+        def evac(engine, out, bank, scale):
+            if engine == "S":
+                nc.scalar.activation(out, bank, COPY, scale=scale)
+            else:
+                nc.vector.tensor_scalar(out, bank, scale, None, MULT)
+
+        def load_rows(engine, tile, scales):
+            rows = scales[0].bitcast(I32)
+            engine.dma_start(out=tile[:].bitcast(I32), in_=rows.unsqueeze(1).to_broadcast([16, 8, rows.shape[1]]))
+
+        def move_rows(engine, plane, rows):
+            for q in range(4):
+                engine.dma_start(out=plane[32 * q : 32 * q + 4, :].bitcast(I32), in_=rows[32 * q : 32 * q + 32 : 8, :].bitcast(I32))
+
+        def deal(engine, dst, src):
+            engine.tensor_copy(dst.rearrange("p (t m) -> p m t", t=PACK), src.rearrange("p (m t) -> p m t", t=PACK))
+
+        def interleave(engine, dst, planes):
+            o = dst[:].rearrange("p (c i t) -> p c t i", i=4, t=PACK)
+            s = planes[:].rearrange("p (t c i) -> p c t i", i=4, t=PACK)
+            if engine == "S":
+                nc.scalar.copy(o, s)
+            else:
+                nc.vector.tensor_copy(o, s)
+
+        d_sc = sb("d_sc", G, U8)
+        x_sc = sb("x_sc", T, U8)
+        x_w = sb("x_w", T, U32)
+        d_w = sb("d_w", G, U32)
+        k1_t = load_list("k1", k1)
+        load_rows(nc.sync, d_sc, d_scales)
+        offs_t = load_list("offs", offs)
+        load_rows(nc.sync, x_sc, x_scales)
+        two_t = load_list("two", two)
+        n1_t = load_list("n1", n1)
+        n2_t = load_list("n2", n2)
+        nc.sync.dma_start(out=d_w[:].bitcast(I32), in_=d_words[0].rearrange("p n t -> p (n t)").bitcast(I32))
+        nc.sync.dma_start(out=x_w[:].bitcast(I32), in_=x_words[0].rearrange("p n t -> p (n t)").bitcast(I32))
+        n3_t = load_list("n3", n3)
+        n4_t = load_list("n4", n4)
+
+        w_sc = [sb("w1_sc", S, U8), sb("w2_sc", S, U8)]
+        w_w = [sb("w1_w", 2 * S, U8), sb("w2_w", 2 * S, U8)]
+        gn_t = sb("gn", PACK, F32)
+        load_rows(nc.gpsimd, w_sc[0], w1_scales)
+        load_rows(nc.gpsimd, w_sc[1], w2_scales)
+        nc.gpsimd.dma_start(out=w_w[0][:].bitcast(I32), in_=w1_words[0].bitcast(I32))
+        nc.gpsimd.dma_start(out=w_w[1][:].bitcast(I32), in_=w2_words[0].bitcast(I32))
+        nc.gpsimd.dma_start(out=gn_t[:], in_=gn.rearrange("(p t) o -> p (t o)", t=PACK))
+
+        first_plane = sb("first_plane", 2 * S, U8)
+        x2_sc = sb("x2_sc", S, U8)
+        w_plane = sb("w_plane", 2 * S, U8)
+        zero(first_plane[:])
+        zero(x2_sc[:])
+        zero(w_plane[:])
+        h = [sb("h%d" % t, S + SPARE, F32) for t in range(PACK)]
+        st = [sb("st%d" % t, S + SPARE, F32) for t in range(PACK)]
+        for t in range(PACK):
+            nc.vector.memset(h[t][:, S:], 0.0)
+            nc.vector.memset(st[t][:, S:], 0.0)
+
+        rows_pool = ctx.enter_context(tc.tile_pool(name="reused", bufs=1))
+        first_rows = rows_pool.tile([P, 2 * S], U8, name="first_rows", offset=3 * S, align_bytes=64)
+        gather("V", first_rows[:, :S], d_sc, k1_t[:])
+        gather("V", first_rows[:, S:], x_sc, offs_t[:])
+        move_rows(nc.scalar, first_plane, first_rows)
+        xq_sc = first_plane[:, S:]
+        dk_w = sb("dk_w", S, U32)
+        gather("V", dk_w[:], d_w, k1_t[:])
+        dk_w_dealt = sb("dk_w_dealt", S, U32)
+        deal(nc.vector, dk_w_dealt[:], dk_w[:])
+        d_plane = sb("d_plane", S, U8)
+        deal(nc.vector, d_plane[:], first_plane[:, :S])
+
+        w_w_dealt = [sb("w1_w_dealt", 2 * S, U8), sb("w2_w_dealt", 2 * S, U8)]
+        w_sc_dealt = sb("w_sc_dealt", 2 * S, U8)
+        for i in range(2):
+            nc.gpsimd.tensor_copy(
+                w_sc_dealt[:, S * i : S * (i + 1)].rearrange("p (t m) -> p t m", t=PACK), w_sc[i][:].rearrange("p (m t) -> p t m", t=PACK)
+            )
+        move_rows(nc.sync, w_plane, w_sc_dealt)
+        for i in range(2):
+            nc.gpsimd.tensor_copy(
+                w_w_dealt[i][:].rearrange("p (t m b) -> p t m b", t=PACK, b=2),
+                w_w[i][:].rearrange("p (m t b) -> p t m b", t=PACK, b=2),
+            )
+
+        h_bank = {}
+
+        def first_product(a):
+            cols = slice(HALF * a, HALF * (a + 1))
+            xq_w = sb("xq_w%d" % a, HALF, U32)
+            gather("V", xq_w[:], x_w, offs_t[:, 16 * a : 16 * (a + 1)])
+            for t in range(PACK):
+                bank = psum.tile([P, HALF], F32, name="bank")
+                rows = slice(P * t, P * (t + 1))
+                nc.tensor.matmul_mx(out=bank[:], lhsT=dk_w_dealt[:, rows].bitcast(FP8X4), lhsT_scale=d_plane[:, rows],
+                                    rhs=xq_w[:].bitcast(FP8X4), rhs_scale=xq_sc[:, cols], start=True, stop=True)
+                h_bank[(a, t)] = bank
+
+        def h_out(engine, a, t):
+            evac(engine, h[t][:, HALF * a : HALF * (a + 1)], h_bank[(a, t)][:], 0.0625)
+
+        x2_w = rows_pool.tile([P, S], U32, name="x2_w", offset=0, align_bytes=64)
+        x2_rows = rows_pool.tile([P, S], U8, name="x2_rows", offset=4 * S, align_bytes=64)
+
+        def second_tokens():
+            gather("V", x2_rows[:], x_sc, two_t[:])
+            move_rows(nc.sync, x2_sc, x2_rows)
+            gather("V", x2_w[:], x_w, two_t[:])
+
+        mb = [sb("mb%d" % t, 2 * S, F32) for t in range(PACK)]
+        mx = [sb("mx%d" % t, S, F32) for t in range(PACK)]
+
+        def members(engine, t, u):
+            gather(engine, mb[t][:, S * u : S * (u + 1)], h[t], n1_t[:, 32 * u : 32 * (u + 1)])
+
+        def largest(t):
+            nc.vector.tensor_tensor(mx[t][:], mb[t][:, 0 : 2 * S : 2], mb[t][:, 1 : 2 * S : 2], MAX)
+
+        def less(t):
+            nc.vector.tensor_tensor(st[t][:, :S], h[t][:, :S], mx[t][:], SUB)
+
+        def span(pieces, a):
+            return pieces[a], pieces[a + 1], pieces[a + 1] - pieces[a]
+
+        n_z = len(Z_CUTS) - 1
+        g2 = {(a, t): sb("g2_%d_%d" % (a, t), span(Z_CUTS, a)[2], F32) for a in range(n_z) for t in range(PACK)}
+        m2 = {(a, t): sb("m_%d_%d" % (a, t), span(Z_CUTS, a)[2], F32) for a in range(n_z) for t in range(PACK)}
+        z_planes = [sb("z_planes%d" % a, PACK * span(Z_CUTS, a)[2], BF16) for a in range(n_z)]
+        z_bf = [sb("z_bf%d" % a, PACK * span(Z_CUTS, a)[2], BF16) for a in range(n_z)]
+        u_t = [sb("u%d" % t, S, F32) for t in range(PACK)]
+        h2_bank = {}
+
+        def look2(engine, a, t):
+            lo, hi, n = span(Z_CUTS, a)
+            gather(engine, g2[(a, t)][:], st[t], n2_t[:, lo // 16 : hi // 16])
+
+        def max2(a, t):
+            lo, hi, n = span(Z_CUTS, a)
+            nc.vector.tensor_tensor(m2[(a, t)][:], st[t][:, lo:hi], g2[(a, t)][:], MAX)
+
+        def gain(engine, a, t):
+            lo, hi, n = span(Z_CUTS, a)
+            evac(engine, z_planes[a][:, n * t : n * (t + 1)], m2[(a, t)][:], gn_t[:, t : t + 1])
+
+        def weave_z(engine, a):
+            interleave(engine, z_bf[a], z_planes[a])
+
+        def second_product(a):
+            lo, hi, n = span(Z_CUTS, a)
+            z_w = sb("z_w%d" % a, n, U32)
+            z_sc = sb("z_sc%d" % a, n, U8)
+            nc.vector.quantize_mx(out=z_w[:].bitcast(FP8X4), scales=z_sc[:], in_=z_bf[a][:])
+            for t in range(PACK):
+                bank = psum.tile([P, n], F32, name="bank")
+                wc = slice(2 * P * t, 2 * P * (t + 1))
+                nc.tensor.matmul_mx(out=bank[:], lhsT=w_w_dealt[1][:, wc].bitcast(FP4X4), lhsT_scale=w_plane[:, S + P * t : S + P * (t + 1)],
+                                    rhs=x2_w[:, lo:hi].bitcast(FP8X4), rhs_scale=x2_sc[:, lo:hi], start=True, stop=False)
+                nc.tensor.matmul_mx(out=bank[:], lhsT=w_w_dealt[0][:, wc].bitcast(FP4X4), lhsT_scale=w_plane[:, P * t : P * (t + 1)],
+                                    rhs=z_w[:].bitcast(FP8X4), rhs_scale=z_sc[:], start=False, stop=True)
+                h2_bank[(a, t)] = bank
+
+        def h2_out(engine, a, t):
+            lo, hi, n = span(Z_CUTS, a)
+            evac(engine, u_t[t][:, lo:hi], h2_bank[(a, t)][:], 0.5)
+
+        g3 = [sb("g3_%d" % t, S, F32) for t in range(PACK)]
+        st2 = [sb("st2_%d" % t, S, F32) for t in range(PACK)]
+
+        def look3(engine, t, a):
+            o = g3[t][:, HALF * a : HALF * (a + 1)]
+            window = u_t[t][:].indirect(n3_t[:, 16 * a : 16 * (a + 1)])
+            if engine == "S":
+                nc.scalar.activation(o, window, COPY, scale=2.0)
+            else:
+                nc.vector.tensor_scalar(o, window, 2.0, 0.0, MULT, ADD)
+
+        def max3(t):
+            nc.vector.scalar_tensor_tensor(st2[t][:], u_t[t][:], 2.0, g3[t][:], MULT, MAX)
+
+        out_rows = out_0.rearrange("(p t) j -> p t j", t=PACK)
+        o_w = sb("o_w", S, U32)
+        o_sc = sb("o_sc", S, U8)
+        words_out = out_1[0].rearrange("p n t -> p (n t)").bitcast(I32)
+        n_o = len(O_CUTS) - 1
+        o_planes = [sb("o_planes%d" % a, PACK * span(O_CUTS, a)[2], F32) for a in range(n_o)]
+        o_bf = [sb("o_bf%d" % a, PACK * span(O_CUTS, a)[2], BF16) for a in range(n_o)]
+        g4 = {}
+
+        def fused4(a, t):
+            lo, hi, n = span(O_CUTS, a)
+            window = st2[t][:].indirect(n4_t[:, lo // 16 : hi // 16])
+            nc.vector.tensor_tensor(o_planes[a][:, n * t : n * (t + 1)], window, u_t[t][:, lo:hi], SUB)
+
+        def look4(a, t):
+            lo, hi, n = span(O_CUTS, a)
+            g4[(a, t)] = sb("g4_%d_%d" % (a, t), n, F32)
+            gather("S", g4[(a, t)][:], st2[t], n4_t[:, lo // 16 : hi // 16])
+
+        def sub4(a, t):
+            lo, hi, n = span(O_CUTS, a)
+            nc.vector.tensor_tensor(o_planes[a][:, n * t : n * (t + 1)], g4[(a, t)][:], u_t[t][:, lo:hi], SUB)
+
+        def store_out(a):
+            lo, hi, n = span(O_CUTS, a)
+            nc.sync.dma_start(out=out_rows[:, :, lo:hi], in_=o_planes[a][:].rearrange("p (t j) -> p t j", t=PACK))
+
+        def weave_o(engine, a):
+            interleave(engine, o_bf[a], o_planes[a])
+
+        def planes_out(a):
+            lo, hi, n = span(O_CUTS, a)
+            nc.vector.quantize_mx(out=o_w[:, lo:hi].bitcast(FP8X4), scales=o_sc[:, lo:hi], in_=o_bf[a][:])
+            nc.sync.dma_start(out=words_out[:, lo:hi], in_=o_w[:, lo:hi].bitcast(I32))
+
+        def scales_out():
+            for q in range(4):
+                engine = nc.scalar if q % 2 else nc.sync
+                engine.dma_start(out=out_2[0, 4 * q : 4 * q + 4, :].bitcast(I32), in_=o_sc[32 * q : 32 * q + 4, :].bitcast(I32))
+
+        first_product(0)
+        h_out("S", 0, 0)
+        h_out("S", 0, 1)
+        h_out("S", 0, 2)
+        h_out("S", 0, 3)
+        first_product(1)
+        second_tokens()
+        h_out("S", 1, 0)
+        h_out("S", 1, 1)
+        h_out("S", 1, 2)
+        h_out("V", 1, 3)
+        members("S", 0, 0)
+        members("S", 0, 1)
+        members("V", 3, 0)
+        members("V", 3, 1)
+        members("S", 1, 0)
+        members("S", 1, 1)
+        members("S", 2, 0)
+        members("S", 2, 1)
+        largest(3)
+        largest(0)
+        less(3)
+        less(0)
+        largest(1)
+        less(1)
+        largest(2)
+        look2("S", 0, 3)
+        look2("S", 0, 0)
+        look2("S", 0, 1)
+        less(2)
+        look2("S", 0, 2)
+        look2("S", 1, 3)
+        look2("S", 1, 0)
+        look2("S", 1, 1)
+        look2("S", 1, 2)
+        max2(0, 3)
+        max2(0, 0)
+        gain("V", 0, 3)
+        max2(0, 1)
+        gain("V", 0, 0)
+        max2(0, 2)
+        gain("V", 0, 1)
+        gain("V", 0, 2)
+        max2(1, 3)
+        weave_z("V", 0)
+        max2(1, 0)
+        second_product(0)
+        gain("V", 1, 3)
+        max2(1, 1)
+        gain("V", 1, 0)
+        max2(1, 2)
+        gain("V", 1, 1)
+        gain("V", 1, 2)
+        h2_out("S", 0, 0)
+        h2_out("S", 0, 1)
+        h2_out("S", 0, 2)
+        h2_out("S", 0, 3)
+        weave_z("V", 1)
+        second_product(1)
+        h2_out("S", 1, 0)
+        h2_out("V", 1, 1)
+        h2_out("S", 1, 2)
+        h2_out("V", 1, 3)
+        look3("S", 0, 0)
+        look3("S", 0, 1)
+        look3("V", 1, 0)
+        look3("V", 1, 1)
+        look3("S", 2, 0)
+        look3("S", 2, 1)
+        look3("S", 3, 0)
+        look3("S", 3, 1)
+        max3(1)
+        max3(0)
+        fused4(0, 1)
+        max3(2)
+        look4(0, 0)
+        max3(3)
+        look4(0, 2)
+        look4(0, 3)
+        look4(1, 1)
+        look4(1, 0)
+        look4(1, 2)
+        look4(1, 3)
+        sub4(0, 0)
+        sub4(0, 2)
+        sub4(0, 3)
+        store_out(0)
+        sub4(1, 1)
+        weave_o("V", 0)
+        sub4(1, 0)
+        planes_out(0)
+        sub4(1, 2)
+        sub4(1, 3)
+        store_out(1)
+        weave_o("V", 1)
+        planes_out(1)
+        scales_out()

@@ -25,6 +25,7 @@ HALF = S // 2
 SPARE = 16
 Z_CUTS = (0, 256, 512)
 O_CUTS = (0, 256, 512)
+HELD = ((1, 0), (1, 1))
 FLOPS = 3 * 2 * 512 * 512 * 512
 
 
@@ -62,14 +63,11 @@ def tile_picked_pqmixghopmhopb_none_po_kernel(
 
         def load_rows(engine, tile, scales):
             rows = scales[0].bitcast(I32)
-            engine.dma_start(out=tile[:].bitcast(I32), in_=rows.unsqueeze(1).to_broadcast([16, 8, rows.shape[1]]))
+            engine.dma_start(out=tile.bitcast(I32), in_=rows.unsqueeze(1).to_broadcast([16, 8, rows.shape[1]]))
 
         def move_rows(engine, plane, rows):
             for q in range(4):
                 engine.dma_start(out=plane[32 * q : 32 * q + 4, :].bitcast(I32), in_=rows[32 * q : 32 * q + 32 : 8, :].bitcast(I32))
-
-        def deal(engine, dst, src):
-            engine.tensor_copy(dst.rearrange("p (t m) -> p m t", t=PACK), src.rearrange("p (m t) -> p m t", t=PACK))
 
         def interleave(engine, dst, planes):
             o = dst[:].rearrange("p (c i t) -> p c t i", i=4, t=PACK)
@@ -84,24 +82,18 @@ def tile_picked_pqmixghopmhopb_none_po_kernel(
         x_w = sb("x_w", T, U32)
         d_w = sb("d_w", G, U32)
         k1_t = load_list("k1", k1)
-        load_rows(nc.sync, d_sc, d_scales)
+        load_rows(nc.sync, d_sc[:], d_scales)
         offs_t = load_list("offs", offs)
-        load_rows(nc.sync, x_sc, x_scales)
+        load_rows(nc.sync, x_sc[:], x_scales)
+        nc.sync.dma_start(out=x_w[:].bitcast(I32), in_=x_words[0].rearrange("p n t -> p (n t)").bitcast(I32))
+        nc.sync.dma_start(out=d_w[:].bitcast(I32), in_=d_words[0].rearrange("p n t -> p (n t)").bitcast(I32))
         two_t = load_list("two", two)
         n1_t = load_list("n1", n1)
         n2_t = load_list("n2", n2)
-        nc.sync.dma_start(out=d_w[:].bitcast(I32), in_=d_words[0].rearrange("p n t -> p (n t)").bitcast(I32))
-        nc.sync.dma_start(out=x_w[:].bitcast(I32), in_=x_words[0].rearrange("p n t -> p (n t)").bitcast(I32))
         n3_t = load_list("n3", n3)
         n4_t = load_list("n4", n4)
 
-        w_sc = [sb("w1_sc", S, U8), sb("w2_sc", S, U8)]
-        w_w = [sb("w1_w", 2 * S, U8), sb("w2_w", 2 * S, U8)]
         gn_t = sb("gn", PACK, F32)
-        load_rows(nc.gpsimd, w_sc[0], w1_scales)
-        load_rows(nc.gpsimd, w_sc[1], w2_scales)
-        nc.gpsimd.dma_start(out=w_w[0][:].bitcast(I32), in_=w1_words[0].bitcast(I32))
-        nc.gpsimd.dma_start(out=w_w[1][:].bitcast(I32), in_=w2_words[0].bitcast(I32))
         nc.gpsimd.dma_start(out=gn_t[:], in_=gn.rearrange("(p t) o -> p (t o)", t=PACK))
 
         first_plane = sb("first_plane", 2 * S, U8)
@@ -116,50 +108,65 @@ def tile_picked_pqmixghopmhopb_none_po_kernel(
             nc.vector.memset(h[t][:, S:], 0.0)
             nc.vector.memset(st[t][:, S:], 0.0)
 
-        rows_pool = ctx.enter_context(tc.tile_pool(name="reused", bufs=1))
-        first_rows = rows_pool.tile([P, 2 * S], U8, name="first_rows", offset=3 * S, align_bytes=64)
-        gather("V", first_rows[:, :S], d_sc, k1_t[:])
-        gather("V", first_rows[:, S:], x_sc, offs_t[:])
+        reused = ctx.enter_context(tc.tile_pool(name="reused", bufs=1))
+
+        def at(name, width, dtype, offset):
+            return reused.tile([P, width], dtype, name=name, offset=offset, align_bytes=64)
+
+        picked_rows = at("picked_rows", 2 * S, U8, 3 * S)
+        first_rows = sb("first_rows", 2 * S, U8)
+        dk_w = at("dk_w", S, U32, 6 * S)
+        gather("V", picked_rows[:, :S], d_sc, k1_t[:])
+        gather("V", picked_rows[:, S:], x_sc, offs_t[:])
+        nc.vector.tensor_copy(first_rows[:, :S].rearrange("p (t m) -> p t m", t=PACK), picked_rows[:, :S].rearrange("p (m t) -> p t m", t=PACK))
+        nc.vector.tensor_copy(first_rows[:, S:].bitcast(I32), picked_rows[:, S:].bitcast(I32))
         move_rows(nc.scalar, first_plane, first_rows)
+        d_plane = first_plane[:, :S]
         xq_sc = first_plane[:, S:]
-        dk_w = sb("dk_w", S, U32)
+        xq_w = sb("xq_w", S, U32)
+        gather("V", xq_w[:], x_w, offs_t[:])
         gather("V", dk_w[:], d_w, k1_t[:])
         dk_w_dealt = sb("dk_w_dealt", S, U32)
-        deal(nc.vector, dk_w_dealt[:], dk_w[:])
-        d_plane = sb("d_plane", S, U8)
-        deal(nc.vector, d_plane[:], first_plane[:, :S])
+        nc.vector.tensor_copy(
+            dk_w_dealt[:].rearrange("p (t c i) -> p c t i", t=PACK, i=4), dk_w[:].rearrange("p (c i t) -> p c t i", t=PACK, i=4)
+        )
 
+        w_words = at("w_words", 4 * S, U8, 0)
+        w_rows = at("w_rows", 2 * S, U8, 4 * S)
+        w_w = [w_words[:, : 2 * S], w_words[:, 2 * S :]]
+        w_sc = [w_rows[:, :S], w_rows[:, S:]]
+        nc.gpsimd.dma_start(out=w_w[0].bitcast(I32), in_=w1_words[0].bitcast(I32))
+        nc.gpsimd.dma_start(out=w_w[1].bitcast(I32), in_=w2_words[0].bitcast(I32))
+        load_rows(nc.gpsimd, w_sc[0], w1_scales)
+        load_rows(nc.gpsimd, w_sc[1], w2_scales)
         w_w_dealt = [sb("w1_w_dealt", 2 * S, U8), sb("w2_w_dealt", 2 * S, U8)]
         w_sc_dealt = sb("w_sc_dealt", 2 * S, U8)
         for i in range(2):
             nc.gpsimd.tensor_copy(
-                w_sc_dealt[:, S * i : S * (i + 1)].rearrange("p (t m) -> p t m", t=PACK), w_sc[i][:].rearrange("p (m t) -> p t m", t=PACK)
+                w_w_dealt[i][:].rearrange("p (t m b) -> p t m b", t=PACK, b=2),
+                w_w[i].rearrange("p (m t b) -> p t m b", t=PACK, b=2),
             )
-        move_rows(nc.sync, w_plane, w_sc_dealt)
         for i in range(2):
             nc.gpsimd.tensor_copy(
-                w_w_dealt[i][:].rearrange("p (t m b) -> p t m b", t=PACK, b=2),
-                w_w[i][:].rearrange("p (m t b) -> p t m b", t=PACK, b=2),
+                w_sc_dealt[:, S * i : S * (i + 1)].rearrange("p (t m) -> p t m", t=PACK), w_sc[i].rearrange("p (m t) -> p t m", t=PACK)
             )
+        move_rows(nc.sync, w_plane, w_sc_dealt)
 
         h_bank = {}
 
-        def first_product(a):
-            cols = slice(HALF * a, HALF * (a + 1))
-            xq_w = sb("xq_w%d" % a, HALF, U32)
-            gather("V", xq_w[:], x_w, offs_t[:, 16 * a : 16 * (a + 1)])
-            for t in range(PACK):
-                bank = psum.tile([P, HALF], F32, name="bank")
+        def first_product():
+            for t in (0, 1, 3, 2):
+                bank = psum.tile([P, S], F32, name="bank")
                 rows = slice(P * t, P * (t + 1))
                 nc.tensor.matmul_mx(out=bank[:], lhsT=dk_w_dealt[:, rows].bitcast(FP8X4), lhsT_scale=d_plane[:, rows],
-                                    rhs=xq_w[:].bitcast(FP8X4), rhs_scale=xq_sc[:, cols], start=True, stop=True)
-                h_bank[(a, t)] = bank
+                                    rhs=xq_w[:].bitcast(FP8X4), rhs_scale=xq_sc, start=True, stop=True)
+                h_bank[t] = bank
 
-        def h_out(engine, a, t):
-            evac(engine, h[t][:, HALF * a : HALF * (a + 1)], h_bank[(a, t)][:], 0.0625)
+        def h_out(engine, t):
+            evac(engine, h[t][:, :S], h_bank[t][:], 0.0625)
 
-        x2_w = rows_pool.tile([P, S], U32, name="x2_w", offset=0, align_bytes=64)
-        x2_rows = rows_pool.tile([P, S], U8, name="x2_rows", offset=4 * S, align_bytes=64)
+        x2_rows = at("x2_rows", S, U8, 6 * S)
+        x2_w = at("x2_w", S, U32, 7 * S)
 
         def second_tokens():
             gather("V", x2_rows[:], x_sc, two_t[:])
@@ -167,7 +174,7 @@ def tile_picked_pqmixghopmhopb_none_po_kernel(
             gather("V", x2_w[:], x_w, two_t[:])
 
         mb = [sb("mb%d" % t, 2 * S, F32) for t in range(PACK)]
-        mx = [sb("mx%d" % t, S, F32) for t in range(PACK)]
+        mx = [at("mx%d" % t, S, F32, 12 * S + 8 * S * t) for t in range(PACK)]
 
         def members(engine, t, u):
             gather(engine, mb[t][:, S * u : S * (u + 1)], h[t], n1_t[:, 32 * u : 32 * (u + 1)])
@@ -182,9 +189,12 @@ def tile_picked_pqmixghopmhopb_none_po_kernel(
             return pieces[a], pieces[a + 1], pieces[a + 1] - pieces[a]
 
         n_z = len(Z_CUTS) - 1
-        g2 = {(a, t): sb("g2_%d_%d" % (a, t), span(Z_CUTS, a)[2], F32) for a in range(n_z) for t in range(PACK)}
-        m2 = {(a, t): sb("m_%d_%d" % (a, t), span(Z_CUTS, a)[2], F32) for a in range(n_z) for t in range(PACK)}
-        z_planes = [sb("z_planes%d" % a, PACK * span(Z_CUTS, a)[2], BF16) for a in range(n_z)]
+        g2 = {(a, t): sb("g2_%d_%d" % (a, t), span(Z_CUTS, a)[2], F32) for a in range(n_z) for t in range(PACK) if (a, t) not in HELD}
+        place = 28 * S - 4 * span(Z_CUTS, HELD[0][0])[2] + (64 if len(HELD) > 2 else 4 * HALF)
+        for a, t in HELD:
+            g2[(a, t)] = at("g2_%d_%d" % (a, t), span(Z_CUTS, a)[2], F32, place)
+            place = place + 4 * span(Z_CUTS, a)[2]
+        m_planes = [sb("m_planes%d" % a, PACK * span(Z_CUTS, a)[2], F32) for a in range(n_z)]
         z_bf = [sb("z_bf%d" % a, PACK * span(Z_CUTS, a)[2], BF16) for a in range(n_z)]
         u_t = [sb("u%d" % t, S, F32) for t in range(PACK)]
         h2_bank = {}
@@ -195,14 +205,16 @@ def tile_picked_pqmixghopmhopb_none_po_kernel(
 
         def max2(a, t):
             lo, hi, n = span(Z_CUTS, a)
-            nc.vector.tensor_tensor(m2[(a, t)][:], st[t][:, lo:hi], g2[(a, t)][:], MAX)
-
-        def gain(engine, a, t):
-            lo, hi, n = span(Z_CUTS, a)
-            evac(engine, z_planes[a][:, n * t : n * (t + 1)], m2[(a, t)][:], gn_t[:, t : t + 1])
+            nc.vector.tensor_tensor(m_planes[a][:, n * t : n * (t + 1)], st[t][:, lo:hi], g2[(a, t)][:], MAX)
 
         def weave_z(engine, a):
-            interleave(engine, z_bf[a], z_planes[a])
+            lo, hi, n = span(Z_CUTS, a)
+            nc.vector.tensor_tensor(
+                z_bf[a][:].rearrange("p (c i t) -> p c t i", i=4, t=PACK),
+                m_planes[a][:].rearrange("p (t c i) -> p c t i", i=4, t=PACK),
+                gn_t[:].unsqueeze(1).unsqueeze(3).to_broadcast([P, n // 4, PACK, 4]),
+                MULT,
+            )
 
         def second_product(a):
             lo, hi, n = span(Z_CUTS, a)
@@ -276,22 +288,17 @@ def tile_picked_pqmixghopmhopb_none_po_kernel(
                 engine = nc.scalar if q % 2 else nc.sync
                 engine.dma_start(out=out_2[0, 4 * q : 4 * q + 4, :].bitcast(I32), in_=o_sc[32 * q : 32 * q + 4, :].bitcast(I32))
 
-        first_product(0)
-        h_out("S", 0, 0)
-        h_out("S", 0, 1)
-        h_out("S", 0, 2)
-        h_out("S", 0, 3)
-        first_product(1)
+        first_product()
         second_tokens()
-        h_out("S", 1, 0)
-        h_out("S", 1, 1)
-        h_out("S", 1, 2)
-        h_out("V", 1, 3)
+        h_out("S", 0)
+        h_out("V", 3)
+        h_out("S", 1)
         members("S", 0, 0)
         members("S", 0, 1)
         members("V", 3, 0)
         members("V", 3, 1)
         members("S", 1, 0)
+        h_out("S", 2)
         members("S", 1, 1)
         members("S", 2, 0)
         members("S", 2, 1)
@@ -300,35 +307,27 @@ def tile_picked_pqmixghopmhopb_none_po_kernel(
         less(3)
         less(0)
         largest(1)
+        look2("V", 0, 3)
         less(1)
         largest(2)
-        look2("S", 0, 3)
         look2("S", 0, 0)
         look2("S", 0, 1)
+        max2(0, 3)
         less(2)
         look2("S", 0, 2)
         look2("S", 1, 3)
         look2("S", 1, 0)
         look2("S", 1, 1)
         look2("S", 1, 2)
-        max2(0, 3)
         max2(0, 0)
-        gain("V", 0, 3)
         max2(0, 1)
-        gain("V", 0, 0)
         max2(0, 2)
-        gain("V", 0, 1)
-        gain("V", 0, 2)
         max2(1, 3)
         weave_z("V", 0)
         max2(1, 0)
         second_product(0)
-        gain("V", 1, 3)
         max2(1, 1)
-        gain("V", 1, 0)
         max2(1, 2)
-        gain("V", 1, 1)
-        gain("V", 1, 2)
         h2_out("S", 0, 0)
         h2_out("S", 0, 1)
         h2_out("S", 0, 2)
@@ -338,11 +337,11 @@ def tile_picked_pqmixghopmhopb_none_po_kernel(
         h2_out("S", 1, 0)
         h2_out("V", 1, 1)
         h2_out("S", 1, 2)
-        h2_out("V", 1, 3)
         look3("S", 0, 0)
         look3("S", 0, 1)
         look3("V", 1, 0)
         look3("V", 1, 1)
+        h2_out("S", 1, 3)
         look3("S", 2, 0)
         look3("S", 2, 1)
         look3("S", 3, 0)
@@ -350,25 +349,21 @@ def tile_picked_pqmixghopmhopb_none_po_kernel(
         max3(1)
         max3(0)
         fused4(0, 1)
+        fused4(0, 0)
         max3(2)
-        look4(0, 0)
+        fused4(0, 2)
         max3(3)
-        look4(0, 2)
-        look4(0, 3)
         look4(1, 1)
         look4(1, 0)
         look4(1, 2)
-        look4(1, 3)
-        sub4(0, 0)
-        sub4(0, 2)
-        sub4(0, 3)
+        fused4(0, 3)
         store_out(0)
+        weave_o("S", 0)
         sub4(1, 1)
-        weave_o("V", 0)
         sub4(1, 0)
-        planes_out(0)
         sub4(1, 2)
-        sub4(1, 3)
+        fused4(1, 3)
+        planes_out(0)
         store_out(1)
         weave_o("V", 1)
         planes_out(1)

@@ -93,6 +93,12 @@ def tile_picked_pqmixghopmhopb_none_po_kernel(
         n3_t = load_list("n3", n3)
         n4_t = load_list("n4", n4)
 
+        w_w = [sb("w1_w", 2 * S, U8)[:], sb("w2_w", 2 * S, U8)[:]]
+        w_sc = [sb("w1_sc", S, U8)[:], sb("w2_sc", S, U8)[:]]
+        nc.gpsimd.dma_start(out=w_w[0].bitcast(I32), in_=w1_words[0].bitcast(I32))
+        nc.gpsimd.dma_start(out=w_w[1].bitcast(I32), in_=w2_words[0].bitcast(I32))
+        load_rows(nc.gpsimd, w_sc[0], w1_scales)
+        load_rows(nc.gpsimd, w_sc[1], w2_scales)
         gn_t = sb("gn", PACK, F32)
         nc.gpsimd.dma_start(out=gn_t[:], in_=gn.rearrange("(p t) o -> p (t o)", t=PACK))
 
@@ -102,7 +108,7 @@ def tile_picked_pqmixghopmhopb_none_po_kernel(
         zero(first_plane[:])
         zero(x2_sc[:])
         zero(w_plane[:])
-        h = [sb("h%d" % t, S + SPARE, F32) for t in range(PACK)]
+        h = [sb("h%d" % t, (S if t == 3 else 2 * S) + SPARE, F32) for t in range(PACK)]
         st = [sb("st%d" % t, S + SPARE, F32) for t in range(PACK)]
         for t in range(PACK):
             nc.vector.memset(h[t][:, S:], 0.0)
@@ -113,8 +119,8 @@ def tile_picked_pqmixghopmhopb_none_po_kernel(
         def at(name, width, dtype, offset):
             return reused.tile([P, width], dtype, name=name, offset=offset, align_bytes=64)
 
-        picked_rows = at("picked_rows", 2 * S, U8, 3 * S)
-        first_rows = sb("first_rows", 2 * S, U8)
+        picked_rows = sb("picked_rows", 2 * S, U8)
+        first_rows = at("first_rows", 2 * S, U8, 3 * S)
         dk_w = at("dk_w", S, U32, 6 * S)
         gather("V", picked_rows[:, :S], d_sc, k1_t[:])
         gather("V", picked_rows[:, S:], x_sc, offs_t[:])
@@ -131,26 +137,19 @@ def tile_picked_pqmixghopmhopb_none_po_kernel(
             dk_w_dealt[:].rearrange("p (t c i) -> p c t i", t=PACK, i=4), dk_w[:].rearrange("p (c i t) -> p c t i", t=PACK, i=4)
         )
 
-        w_words = at("w_words", 4 * S, U8, 0)
-        w_rows = at("w_rows", 2 * S, U8, 4 * S)
-        w_w = [w_words[:, : 2 * S], w_words[:, 2 * S :]]
-        w_sc = [w_rows[:, :S], w_rows[:, S:]]
-        nc.gpsimd.dma_start(out=w_w[0].bitcast(I32), in_=w1_words[0].bitcast(I32))
-        nc.gpsimd.dma_start(out=w_w[1].bitcast(I32), in_=w2_words[0].bitcast(I32))
-        load_rows(nc.gpsimd, w_sc[0], w1_scales)
-        load_rows(nc.gpsimd, w_sc[1], w2_scales)
-        w_w_dealt = [sb("w1_w_dealt", 2 * S, U8), sb("w2_w_dealt", 2 * S, U8)]
-        w_sc_dealt = sb("w_sc_dealt", 2 * S, U8)
-        for i in range(2):
-            nc.gpsimd.tensor_copy(
-                w_w_dealt[i][:].rearrange("p (t m b) -> p t m b", t=PACK, b=2),
-                w_w[i].rearrange("p (m t b) -> p t m b", t=PACK, b=2),
-            )
+        w_words_dealt = at("w_words_dealt", 4 * S, U8, 0)
+        w_w_dealt = [w_words_dealt[:, : 2 * S], w_words_dealt[:, 2 * S :]]
+        w_sc_dealt = at("w_sc_dealt", 2 * S, U8, 4 * S)
         for i in range(2):
             nc.gpsimd.tensor_copy(
                 w_sc_dealt[:, S * i : S * (i + 1)].rearrange("p (t m) -> p t m", t=PACK), w_sc[i].rearrange("p (m t) -> p t m", t=PACK)
             )
         move_rows(nc.sync, w_plane, w_sc_dealt)
+        for i in range(2):
+            nc.gpsimd.tensor_copy(
+                w_w_dealt[i].rearrange("p (t m b) -> p t m b", t=PACK, b=2),
+                w_w[i].rearrange("p (m t b) -> p t m b", t=PACK, b=2),
+            )
 
         h_bank = {}
 
@@ -178,6 +177,9 @@ def tile_picked_pqmixghopmhopb_none_po_kernel(
 
         def members(engine, t, u):
             gather(engine, mb[t][:, S * u : S * (u + 1)], h[t], n1_t[:, 32 * u : 32 * (u + 1)])
+
+        def all_members(t):
+            gather("S", mb[t][:], h[t], n1_t[:])
 
         def largest(t):
             nc.vector.tensor_tensor(mx[t][:], mb[t][:, 0 : 2 * S : 2], mb[t][:, 1 : 2 * S : 2], MAX)
@@ -289,82 +291,80 @@ def tile_picked_pqmixghopmhopb_none_po_kernel(
                 engine.dma_start(out=out_2[0, 4 * q : 4 * q + 4, :].bitcast(I32), in_=o_sc[32 * q : 32 * q + 4, :].bitcast(I32))
 
         first_product()
-        second_tokens()
         h_out("S", 0)
-        h_out("V", 3)
         h_out("S", 1)
-        members("S", 0, 0)
-        members("S", 0, 1)
+        all_members(0)
+        second_tokens()
+        h_out("V", 3)
+        h_out("V", 2)
+        all_members(1)
         members("V", 3, 0)
         members("V", 3, 1)
-        members("S", 1, 0)
-        h_out("S", 2)
-        members("S", 1, 1)
-        members("S", 2, 0)
-        members("S", 2, 1)
-        largest(3)
+        all_members(2)
         largest(0)
+        largest(3)
+        largest(1)
         less(3)
         less(0)
-        largest(1)
-        look2("V", 0, 3)
         less(1)
         largest(2)
+        look2("S", 0, 3)
         look2("S", 0, 0)
         look2("S", 0, 1)
-        max2(0, 3)
         less(2)
         look2("S", 0, 2)
         look2("S", 1, 3)
         look2("S", 1, 0)
         look2("S", 1, 1)
         look2("S", 1, 2)
+        max2(0, 3)
         max2(0, 0)
         max2(0, 1)
         max2(0, 2)
         max2(1, 3)
         weave_z("V", 0)
         max2(1, 0)
-        second_product(0)
         max2(1, 1)
+        second_product(0)
         max2(1, 2)
+        weave_z("V", 1)
         h2_out("S", 0, 0)
         h2_out("S", 0, 1)
         h2_out("S", 0, 2)
         h2_out("S", 0, 3)
-        weave_z("V", 1)
         second_product(1)
-        h2_out("S", 1, 0)
-        h2_out("V", 1, 1)
-        h2_out("S", 1, 2)
+        h2_out("V", 1, 0)
+        h2_out("S", 1, 1)
+        h2_out("V", 1, 2)
         look3("S", 0, 0)
-        look3("S", 0, 1)
+        look3("V", 0, 1)
+        look3("S", 1, 1)
         look3("V", 1, 0)
-        look3("V", 1, 1)
         h2_out("S", 1, 3)
-        look3("S", 2, 0)
-        look3("S", 2, 1)
         look3("S", 3, 0)
         look3("S", 3, 1)
-        max3(1)
+        look3("S", 2, 0)
+        look3("S", 2, 1)
         max3(0)
-        fused4(0, 1)
+        max3(1)
         fused4(0, 0)
-        max3(2)
-        fused4(0, 2)
-        max3(3)
-        look4(1, 1)
+        fused4(0, 1)
         look4(1, 0)
+        look4(1, 1)
+        max3(3)
+        max3(2)
+        look4(1, 3)
         look4(1, 2)
+        sub4(1, 0)
+        fused4(0, 2)
         fused4(0, 3)
         store_out(0)
         weave_o("S", 0)
         sub4(1, 1)
-        sub4(1, 0)
+        sub4(1, 3)
         sub4(1, 2)
-        fused4(1, 3)
-        planes_out(0)
         store_out(1)
         weave_o("V", 1)
+        planes_out(0)
         planes_out(1)
         scales_out()

@@ -11,21 +11,24 @@ U8 = mybir.dt.uint8
 FP8X4 = mybir.dt.float8_e4m3fn_x4
 FP4X4 = mybir.dt.float4_e2m1fn_x4
 COPY = mybir.ActivationFunctionType.Copy
+ADD = mybir.AluOpType.add
 MAX = mybir.AluOpType.max
 MULT = mybir.AluOpType.mult
-ADD = mybir.AluOpType.add
 SUB = mybir.AluOpType.subtract
 
 P = 128
 PACK = 4
 S = 512
-T = 1024
-G = 2048
+TOKENS = 1024
+CODEWORDS = 2048
+BLOCKS = 16
 HALF = S // 2
+GROUP = 16
+LINE = 4
 SPARE = 16
-Z_CUTS = (0, 256, 512)
-O_CUTS = (0, 256, 512)
-HELD = ((1, 0), (1, 1))
+VECTOR_TILE = 3
+LAST_TILE = 2
+EARLY_TILES = (3, 0, 1)
 FLOPS = 3 * 2 * 512 * 512 * 512
 
 
@@ -36,335 +39,277 @@ def tile_picked_pqmixghopmhopb_none_po_kernel(
     nc = tc.nc
     with ExitStack() as ctx:
         keep = ctx.enter_context(tc.tile_pool(name="keep", bufs=1))
+        reused = ctx.enter_context(tc.tile_pool(name="reused", bufs=1))
         psum = ctx.enter_context(tc.psum_pool(name="psum", bufs=8))
 
         def sb(name, width, dtype):
             return keep.tile([P, width], dtype, name=name, align_bytes=64)
 
+        def placed(name, width, dtype, offset):
+            return reused.tile([P, width], dtype, name=name, offset=offset, align_bytes=64)
+
+        def half(a):
+            return slice(HALF * a, HALF * (a + 1))
+
+        def slot(t):
+            return slice(HALF * t, HALF * (t + 1))
+
+        def half_entries(list_tile, a):
+            return list_tile[:, HALF // GROUP * a : HALF // GROUP * (a + 1)]
+
         def load_list(name, src):
-            t = keep.tile([P, src.shape[1]], U16, name=name)
-            nc.sync.dma_start(t[:], src)
-            return t
+            list_tile = keep.tile([P, src.shape[1]], U16, name=name)
+            nc.sync.dma_start(list_tile[:], src)
+            return list_tile
 
-        def zero(ap):
-            nc.vector.memset(ap.bitcast(I32), 0)
+        def load_words(engine, tile, src):
+            engine.dma_start(out=tile[:].bitcast(I32), in_=src.bitcast(I32))
 
-        def gather(engine, out, window, offsets):
-            if engine == "S":
-                nc.scalar.activation(out, window[:].indirect(offsets), COPY)
-            else:
-                nc.vector.tensor_copy(out, window[:].indirect(offsets))
-
-        def evac(engine, out, bank, scale):
-            if engine == "S":
-                nc.scalar.activation(out, bank, COPY, scale=scale)
-            else:
-                nc.vector.tensor_scalar(out, bank, scale, None, MULT)
-
-        def load_rows(engine, tile, scales):
+        def load_scale_rows(engine, tile, scales):
             rows = scales[0].bitcast(I32)
-            engine.dma_start(out=tile.bitcast(I32), in_=rows.unsqueeze(1).to_broadcast([16, 8, rows.shape[1]]))
+            engine.dma_start(out=tile[:].bitcast(I32), in_=rows.unsqueeze(1).to_broadcast([BLOCKS, P // BLOCKS, rows.shape[1]]))
 
-        def move_rows(engine, plane, rows):
+        def rows_to_plane(engine, plane, rows):
             for q in range(4):
                 engine.dma_start(out=plane[32 * q : 32 * q + 4, :].bitcast(I32), in_=rows[32 * q : 32 * q + 32 : 8, :].bitcast(I32))
 
-        def interleave(engine, dst, planes):
-            o = dst[:].rearrange("p (c i t) -> p c t i", i=4, t=PACK)
-            s = planes[:].rearrange("p (t c i) -> p c t i", i=4, t=PACK)
-            if engine == "S":
-                nc.scalar.copy(o, s)
-            else:
-                nc.vector.tensor_copy(o, s)
+        def deal_bytes(engine, dst, src):
+            engine.tensor_copy(dst.rearrange("p (t m) -> p t m", t=PACK), src.rearrange("p (m t) -> p t m", t=PACK))
 
-        d_sc = sb("d_sc", G, U8)
-        x_sc = sb("x_sc", T, U8)
-        x_w = sb("x_w", T, U32)
-        d_w = sb("d_w", G, U32)
-        k1_t = load_list("k1", k1)
-        load_rows(nc.sync, d_sc[:], d_scales)
-        offs_t = load_list("offs", offs)
-        load_rows(nc.sync, x_sc[:], x_scales)
-        nc.sync.dma_start(out=x_w[:].bitcast(I32), in_=x_words[0].rearrange("p n t -> p (n t)").bitcast(I32))
-        nc.sync.dma_start(out=d_w[:].bitcast(I32), in_=d_words[0].rearrange("p n t -> p (n t)").bitcast(I32))
-        two_t = load_list("two", two)
-        n1_t = load_list("n1", n1)
-        n2_t = load_list("n2", n2)
-        n3_t = load_list("n3", n3)
-        n4_t = load_list("n4", n4)
+        def woven(tile):
+            return tile[:].rearrange("p (c i t) -> p c t i", i=LINE, t=PACK)
 
-        w_w = [sb("w1_w", 2 * S, U8)[:], sb("w2_w", 2 * S, U8)[:]]
-        w_sc = [sb("w1_sc", S, U8)[:], sb("w2_sc", S, U8)[:]]
-        nc.gpsimd.dma_start(out=w_w[0].bitcast(I32), in_=w1_words[0].bitcast(I32))
-        nc.gpsimd.dma_start(out=w_w[1].bitcast(I32), in_=w2_words[0].bitcast(I32))
-        load_rows(nc.gpsimd, w_sc[0], w1_scales)
-        load_rows(nc.gpsimd, w_sc[1], w2_scales)
-        gn_t = sb("gn", PACK, F32)
-        nc.gpsimd.dma_start(out=gn_t[:], in_=gn.rearrange("(p t) o -> p (t o)", t=PACK))
+        def side_by_side(tile):
+            return tile[:].rearrange("p (t c i) -> p c t i", i=LINE, t=PACK)
+
+        def vector_gather(out, window, offsets):
+            nc.vector.tensor_copy(out, window[:].indirect(offsets))
+
+        def scalar_gather(out, window, offsets):
+            nc.scalar.activation(out, window[:].indirect(offsets), COPY)
+
+        def vector_empties(out, bank, factor):
+            nc.vector.tensor_scalar(out, bank[:], factor, None, MULT)
+
+        def scalar_empties(out, bank, factor):
+            nc.scalar.activation(out, bank[:], COPY, scale=factor)
+
+        d_rows = sb("d_rows", CODEWORDS, U8)
+        x_rows = sb("x_rows", TOKENS, U8)
+        x_table = sb("x_table", TOKENS, U32)
+        d_table = sb("d_table", CODEWORDS, U32)
+        k1_list = load_list("k1_list", k1)
+        load_scale_rows(nc.sync, d_rows, d_scales)
+        offs_list = load_list("offs_list", offs)
+        load_scale_rows(nc.sync, x_rows, x_scales)
+        load_words(nc.sync, x_table, x_words[0].rearrange("p n t -> p (n t)"))
+        load_words(nc.sync, d_table, d_words[0].rearrange("p n t -> p (n t)"))
+        two_list = load_list("two_list", two)
+        n1_list = load_list("n1_list", n1)
+        n2_list = load_list("n2_list", n2)
+        n3_list = load_list("n3_list", n3)
+        n4_list = load_list("n4_list", n4)
+
+        w_words = [sb("w1_words", 2 * S, U8), sb("w2_words", 2 * S, U8)]
+        w_rows = [sb("w1_rows", S, U8), sb("w2_rows", S, U8)]
+        load_words(nc.gpsimd, w_words[0], w1_words[0])
+        load_words(nc.gpsimd, w_words[1], w2_words[0])
+        load_scale_rows(nc.gpsimd, w_rows[0], w1_scales)
+        load_scale_rows(nc.gpsimd, w_rows[1], w2_scales)
+        gain = sb("gain", PACK, F32)
+        nc.gpsimd.dma_start(out=gain[:], in_=gn.rearrange("(p t) o -> p (t o)", t=PACK))
 
         first_plane = sb("first_plane", 2 * S, U8)
-        x2_sc = sb("x2_sc", S, U8)
+        two_plane = sb("two_plane", S, U8)
         w_plane = sb("w_plane", 2 * S, U8)
-        zero(first_plane[:])
-        zero(x2_sc[:])
-        zero(w_plane[:])
-        h = [sb("h%d" % t, (S if t == 3 else 2 * S) + SPARE, F32) for t in range(PACK)]
+        for plane in (first_plane, two_plane, w_plane):
+            nc.vector.memset(plane[:].bitcast(I32), 0)
+        h = [sb("h%d" % t, (S if t == VECTOR_TILE else 2 * S) + SPARE, F32) for t in range(PACK)]
         st = [sb("st%d" % t, S + SPARE, F32) for t in range(PACK)]
         for t in range(PACK):
             nc.vector.memset(h[t][:, S:], 0.0)
             nc.vector.memset(st[t][:, S:], 0.0)
 
-        reused = ctx.enter_context(tc.tile_pool(name="reused", bufs=1))
-
-        def at(name, width, dtype, offset):
-            return reused.tile([P, width], dtype, name=name, offset=offset, align_bytes=64)
-
-        picked_rows = sb("picked_rows", 2 * S, U8)
-        first_rows = at("first_rows", 2 * S, U8, 3 * S)
-        dk_w = at("dk_w", S, U32, 6 * S)
-        gather("V", picked_rows[:, :S], d_sc, k1_t[:])
-        gather("V", picked_rows[:, S:], x_sc, offs_t[:])
-        nc.vector.tensor_copy(first_rows[:, :S].rearrange("p (t m) -> p t m", t=PACK), picked_rows[:, :S].rearrange("p (m t) -> p t m", t=PACK))
+        picked_rows = placed("picked_rows", 2 * S, U8, 16 * S)
+        first_rows = placed("first_rows", 2 * S, U8, 3 * S)
+        dk_words = placed("dk_words", S, U32, 6 * S)
+        vector_gather(picked_rows[:, :S], d_rows, k1_list[:])
+        vector_gather(picked_rows[:, S:], x_rows, offs_list[:])
+        deal_bytes(nc.vector, first_rows[:, :S], picked_rows[:, :S])
         nc.vector.tensor_copy(first_rows[:, S:].bitcast(I32), picked_rows[:, S:].bitcast(I32))
-        move_rows(nc.scalar, first_plane, first_rows)
-        d_plane = first_plane[:, :S]
-        xq_sc = first_plane[:, S:]
-        xq_w = sb("xq_w", S, U32)
-        gather("V", xq_w[:], x_w, offs_t[:])
-        gather("V", dk_w[:], d_w, k1_t[:])
-        dk_w_dealt = sb("dk_w_dealt", S, U32)
-        nc.vector.tensor_copy(
-            dk_w_dealt[:].rearrange("p (t c i) -> p c t i", t=PACK, i=4), dk_w[:].rearrange("p (c i t) -> p c t i", t=PACK, i=4)
-        )
+        rows_to_plane(nc.scalar, first_plane, first_rows)
+        xq_words = placed("xq_words", S, U32, 16 * S)
+        vector_gather(xq_words[:], x_table, offs_list[:])
+        vector_gather(dk_words[:], d_table, k1_list[:])
+        dk_dealt = sb("dk_dealt", S, U32)
+        nc.vector.tensor_copy(side_by_side(dk_dealt), woven(dk_words))
 
-        w_words_dealt = at("w_words_dealt", 4 * S, U8, 0)
-        w_w_dealt = [w_words_dealt[:, : 2 * S], w_words_dealt[:, 2 * S :]]
-        w_sc_dealt = at("w_sc_dealt", 2 * S, U8, 4 * S)
+        w_words_dealt = placed("w_words_dealt", 4 * S, U8, 0)
+        w_rows_dealt = placed("w_rows_dealt", 2 * S, U8, 4 * S)
+        for i in range(2):
+            deal_bytes(nc.gpsimd, w_rows_dealt[:, S * i : S * (i + 1)], w_rows[i][:])
+        rows_to_plane(nc.sync, w_plane, w_rows_dealt)
         for i in range(2):
             nc.gpsimd.tensor_copy(
-                w_sc_dealt[:, S * i : S * (i + 1)].rearrange("p (t m) -> p t m", t=PACK), w_sc[i].rearrange("p (m t) -> p t m", t=PACK)
-            )
-        move_rows(nc.sync, w_plane, w_sc_dealt)
-        for i in range(2):
-            nc.gpsimd.tensor_copy(
-                w_w_dealt[i].rearrange("p (t m b) -> p t m b", t=PACK, b=2),
-                w_w[i].rearrange("p (m t b) -> p t m b", t=PACK, b=2),
+                w_words_dealt[:, 2 * S * i : 2 * S * (i + 1)].rearrange("p (t m b) -> p t m b", t=PACK, b=2),
+                w_words[i][:].rearrange("p (m t b) -> p t m b", t=PACK, b=2),
             )
 
         h_bank = {}
-
-        def first_product():
-            for t in (0, 1, 3, 2):
-                bank = psum.tile([P, S], F32, name="bank")
-                rows = slice(P * t, P * (t + 1))
-                nc.tensor.matmul_mx(out=bank[:], lhsT=dk_w_dealt[:, rows].bitcast(FP8X4), lhsT_scale=d_plane[:, rows],
-                                    rhs=xq_w[:].bitcast(FP8X4), rhs_scale=xq_sc, start=True, stop=True)
-                h_bank[t] = bank
-
-        def h_out(engine, t):
-            evac(engine, h[t][:, :S], h_bank[t][:], 0.0625)
-
-        x2_rows = at("x2_rows", S, U8, 6 * S)
-        x2_w = at("x2_w", S, U32, 7 * S)
-
-        def second_tokens():
-            gather("V", x2_rows[:], x_sc, two_t[:])
-            move_rows(nc.sync, x2_sc, x2_rows)
-            gather("V", x2_w[:], x_w, two_t[:])
-
-        mb = [sb("mb%d" % t, 2 * S, F32) for t in range(PACK)]
-        mx = [at("mx%d" % t, S, F32, 12 * S + 8 * S * t) for t in range(PACK)]
-
-        def members(engine, t, u):
-            gather(engine, mb[t][:, S * u : S * (u + 1)], h[t], n1_t[:, 32 * u : 32 * (u + 1)])
-
-        def all_members(t):
-            gather("S", mb[t][:], h[t], n1_t[:])
-
-        def largest(t):
-            nc.vector.tensor_tensor(mx[t][:], mb[t][:, 0 : 2 * S : 2], mb[t][:, 1 : 2 * S : 2], MAX)
-
-        def less(t):
-            nc.vector.tensor_tensor(st[t][:, :S], h[t][:, :S], mx[t][:], SUB)
-
-        def span(pieces, a):
-            return pieces[a], pieces[a + 1], pieces[a + 1] - pieces[a]
-
-        n_z = len(Z_CUTS) - 1
-        g2 = {(a, t): sb("g2_%d_%d" % (a, t), span(Z_CUTS, a)[2], F32) for a in range(n_z) for t in range(PACK) if (a, t) not in HELD}
-        place = 28 * S - 4 * span(Z_CUTS, HELD[0][0])[2] + (64 if len(HELD) > 2 else 4 * HALF)
-        for a, t in HELD:
-            g2[(a, t)] = at("g2_%d_%d" % (a, t), span(Z_CUTS, a)[2], F32, place)
-            place = place + 4 * span(Z_CUTS, a)[2]
-        m_planes = [sb("m_planes%d" % a, PACK * span(Z_CUTS, a)[2], F32) for a in range(n_z)]
-        z_bf = [sb("z_bf%d" % a, PACK * span(Z_CUTS, a)[2], BF16) for a in range(n_z)]
-        u_t = [sb("u%d" % t, S, F32) for t in range(PACK)]
-        h2_bank = {}
-
-        def look2(engine, a, t):
-            lo, hi, n = span(Z_CUTS, a)
-            gather(engine, g2[(a, t)][:], st[t], n2_t[:, lo // 16 : hi // 16])
-
-        def max2(a, t):
-            lo, hi, n = span(Z_CUTS, a)
-            nc.vector.tensor_tensor(m_planes[a][:, n * t : n * (t + 1)], st[t][:, lo:hi], g2[(a, t)][:], MAX)
-
-        def weave_z(engine, a):
-            lo, hi, n = span(Z_CUTS, a)
-            nc.vector.tensor_tensor(
-                z_bf[a][:].rearrange("p (c i t) -> p c t i", i=4, t=PACK),
-                m_planes[a][:].rearrange("p (t c i) -> p c t i", i=4, t=PACK),
-                gn_t[:].unsqueeze(1).unsqueeze(3).to_broadcast([P, n // 4, PACK, 4]),
-                MULT,
+        for t in (0, 1, VECTOR_TILE, LAST_TILE):
+            h_bank[t] = psum.tile([P, S], F32, name="bank")
+            nc.tensor.matmul_mx(
+                out=h_bank[t][:], lhsT=dk_dealt[:, P * t : P * (t + 1)].bitcast(FP8X4), lhsT_scale=first_plane[:, P * t : P * (t + 1)],
+                rhs=xq_words[:].bitcast(FP8X4), rhs_scale=first_plane[:, S:], start=True, stop=True,
             )
 
+        mb = [sb("mb%d" % t, 2 * S, F32) for t in range(PACK)]
+        scalar_empties(h[0][:, :S], h_bank[0], 0.0625)
+        scalar_empties(h[1][:, :S], h_bank[1], 0.0625)
+        scalar_gather(mb[0][:], h[0], n1_list[:])
+
+        two_rows = placed("two_rows", S, U8, 6 * S)
+        two_words = placed("two_words", S, U32, 7 * S)
+        vector_gather(two_rows[:], x_rows, two_list[:])
+        rows_to_plane(nc.sync, two_plane, two_rows)
+        vector_gather(two_words[:], x_table, two_list[:])
+
+        vector_empties(h[VECTOR_TILE][:, :S], h_bank[VECTOR_TILE], 0.0625)
+        vector_empties(h[LAST_TILE][:, :S], h_bank[LAST_TILE], 0.0625)
+        scalar_gather(mb[1][:], h[1], n1_list[:])
+        for a in range(2):
+            vector_gather(mb[VECTOR_TILE][:, S * a : S * (a + 1)], h[VECTOR_TILE], n1_list[:, S // GROUP * a : S // GROUP * (a + 1)])
+        scalar_gather(mb[LAST_TILE][:], h[LAST_TILE], n1_list[:])
+
+        mx = [placed("mx_last", S, F32, 12 * S) if t == LAST_TILE else sb("mx%d" % t, S, F32) for t in range(PACK)]
+        on_mx_last = {(1, 0): 12 * S, (1, 1): 14 * S}
+        st_n2 = {
+            (a, t): placed("st_n2_%d%d" % (a, t), HALF, F32, on_mx_last[(a, t)]) if (a, t) in on_mx_last else sb("st_n2_%d%d" % (a, t), HALF, F32)
+            for a in range(2)
+            for t in range(PACK)
+        }
+        larger = [sb("larger%d" % a, PACK * HALF, F32) for a in range(2)]
+        z_woven = [sb("z_woven%d" % a, PACK * HALF, BF16) for a in range(2)]
+        h2_bank = {}
+
+        def larger_member(t):
+            nc.vector.tensor_tensor(mx[t][:], mb[t][:, 0 : 2 * S : 2], mb[t][:, 1 : 2 * S : 2], MAX)
+
+        def make_st(t):
+            nc.vector.tensor_tensor(st[t][:, :S], h[t][:, :S], mx[t][:], SUB)
+
+        def look_up_n2(a, t):
+            scalar_gather(st_n2[(a, t)][:], st[t], half_entries(n2_list, a))
+
+        def make_larger(a, t):
+            nc.vector.tensor_tensor(larger[a][:, slot(t)], st[t][:, half(a)], st_n2[(a, t)][:], MAX)
+
+        def make_z(a):
+            spread = gain[:].unsqueeze(1).unsqueeze(3).to_broadcast([P, HALF // LINE, PACK, LINE])
+            nc.vector.tensor_tensor(woven(z_woven[a]), side_by_side(larger[a]), spread, MULT)
+
         def second_product(a):
-            lo, hi, n = span(Z_CUTS, a)
-            z_w = sb("z_w%d" % a, n, U32)
-            z_sc = sb("z_sc%d" % a, n, U8)
-            nc.vector.quantize_mx(out=z_w[:].bitcast(FP8X4), scales=z_sc[:], in_=z_bf[a][:])
+            z_words = sb("z_words%d" % a, HALF, U32)
+            z_plane = sb("z_plane%d" % a, HALF, U8)
+            nc.vector.quantize_mx(out=z_words[:].bitcast(FP8X4), scales=z_plane[:], in_=z_woven[a][:])
             for t in range(PACK):
-                bank = psum.tile([P, n], F32, name="bank")
-                wc = slice(2 * P * t, 2 * P * (t + 1))
-                nc.tensor.matmul_mx(out=bank[:], lhsT=w_w_dealt[1][:, wc].bitcast(FP4X4), lhsT_scale=w_plane[:, S + P * t : S + P * (t + 1)],
-                                    rhs=x2_w[:, lo:hi].bitcast(FP8X4), rhs_scale=x2_sc[:, lo:hi], start=True, stop=False)
-                nc.tensor.matmul_mx(out=bank[:], lhsT=w_w_dealt[0][:, wc].bitcast(FP4X4), lhsT_scale=w_plane[:, P * t : P * (t + 1)],
-                                    rhs=z_w[:].bitcast(FP8X4), rhs_scale=z_sc[:], start=False, stop=True)
-                h2_bank[(a, t)] = bank
+                h2_bank[(a, t)] = psum.tile([P, HALF], F32, name="bank")
+                operands = ((1, two_words[:, half(a)], two_plane[:, half(a)]), (0, z_words[:], z_plane[:]))
+                for i, words, plane in operands:
+                    first = S * i + P * t
+                    nc.tensor.matmul_mx(
+                        out=h2_bank[(a, t)][:], lhsT=w_words_dealt[:, 2 * first : 2 * (first + P)].bitcast(FP4X4),
+                        lhsT_scale=w_plane[:, first : first + P], rhs=words.bitcast(FP8X4), rhs_scale=plane,
+                        start=(i == 1), stop=(i == 0),
+                    )
 
-        def h2_out(engine, a, t):
-            lo, hi, n = span(Z_CUTS, a)
-            evac(engine, u_t[t][:, lo:hi], h2_bank[(a, t)][:], 0.5)
-
-        g3 = [sb("g3_%d" % t, S, F32) for t in range(PACK)]
-        st2 = [sb("st2_%d" % t, S, F32) for t in range(PACK)]
-
-        def look3(engine, t, a):
-            o = g3[t][:, HALF * a : HALF * (a + 1)]
-            window = u_t[t][:].indirect(n3_t[:, 16 * a : 16 * (a + 1)])
-            if engine == "S":
-                nc.scalar.activation(o, window, COPY, scale=2.0)
-            else:
-                nc.vector.tensor_scalar(o, window, 2.0, 0.0, MULT, ADD)
-
-        def max3(t):
-            nc.vector.scalar_tensor_tensor(st2[t][:], u_t[t][:], 2.0, g3[t][:], MULT, MAX)
-
-        out_rows = out_0.rearrange("(p t) j -> p t j", t=PACK)
-        o_w = sb("o_w", S, U32)
-        o_sc = sb("o_sc", S, U8)
-        words_out = out_1[0].rearrange("p n t -> p (n t)").bitcast(I32)
-        n_o = len(O_CUTS) - 1
-        o_planes = [sb("o_planes%d" % a, PACK * span(O_CUTS, a)[2], F32) for a in range(n_o)]
-        o_bf = [sb("o_bf%d" % a, PACK * span(O_CUTS, a)[2], BF16) for a in range(n_o)]
-        g4 = {}
-
-        def fused4(a, t):
-            lo, hi, n = span(O_CUTS, a)
-            window = st2[t][:].indirect(n4_t[:, lo // 16 : hi // 16])
-            nc.vector.tensor_tensor(o_planes[a][:, n * t : n * (t + 1)], window, u_t[t][:, lo:hi], SUB)
-
-        def look4(a, t):
-            lo, hi, n = span(O_CUTS, a)
-            g4[(a, t)] = sb("g4_%d_%d" % (a, t), n, F32)
-            gather("S", g4[(a, t)][:], st2[t], n4_t[:, lo // 16 : hi // 16])
-
-        def sub4(a, t):
-            lo, hi, n = span(O_CUTS, a)
-            nc.vector.tensor_tensor(o_planes[a][:, n * t : n * (t + 1)], g4[(a, t)][:], u_t[t][:, lo:hi], SUB)
-
-        def store_out(a):
-            lo, hi, n = span(O_CUTS, a)
-            nc.sync.dma_start(out=out_rows[:, :, lo:hi], in_=o_planes[a][:].rearrange("p (t j) -> p t j", t=PACK))
-
-        def weave_o(engine, a):
-            interleave(engine, o_bf[a], o_planes[a])
-
-        def planes_out(a):
-            lo, hi, n = span(O_CUTS, a)
-            nc.vector.quantize_mx(out=o_w[:, lo:hi].bitcast(FP8X4), scales=o_sc[:, lo:hi], in_=o_bf[a][:])
-            nc.sync.dma_start(out=words_out[:, lo:hi], in_=o_w[:, lo:hi].bitcast(I32))
-
-        def scales_out():
-            for q in range(4):
-                engine = nc.scalar if q % 2 else nc.sync
-                engine.dma_start(out=out_2[0, 4 * q : 4 * q + 4, :].bitcast(I32), in_=o_sc[32 * q : 32 * q + 4, :].bitcast(I32))
-
-        first_product()
-        h_out("S", 0)
-        h_out("S", 1)
-        all_members(0)
-        second_tokens()
-        h_out("V", 3)
-        h_out("V", 2)
-        all_members(1)
-        members("V", 3, 0)
-        members("V", 3, 1)
-        all_members(2)
-        largest(0)
-        largest(3)
-        largest(1)
-        less(3)
-        less(0)
-        less(1)
-        largest(2)
-        look2("S", 0, 3)
-        look2("S", 0, 0)
-        look2("S", 0, 1)
-        less(2)
-        look2("S", 0, 2)
-        look2("S", 1, 3)
-        look2("S", 1, 0)
-        look2("S", 1, 1)
-        look2("S", 1, 2)
-        max2(0, 3)
-        max2(0, 0)
-        max2(0, 1)
-        max2(0, 2)
-        max2(1, 3)
-        weave_z("V", 0)
-        max2(1, 0)
-        max2(1, 1)
+        for t in (0, VECTOR_TILE, 1):
+            larger_member(t)
+        for t in EARLY_TILES:
+            make_st(t)
+        larger_member(LAST_TILE)
+        for t in EARLY_TILES:
+            look_up_n2(0, t)
+        make_st(LAST_TILE)
+        look_up_n2(0, LAST_TILE)
+        for t in EARLY_TILES + (LAST_TILE,):
+            look_up_n2(1, t)
+        for t in EARLY_TILES + (LAST_TILE,):
+            make_larger(0, t)
+        make_larger(1, EARLY_TILES[0])
+        make_z(0)
+        for t in EARLY_TILES[1:]:
+            make_larger(1, t)
         second_product(0)
-        max2(1, 2)
-        weave_z("V", 1)
-        h2_out("S", 0, 0)
-        h2_out("S", 0, 1)
-        h2_out("S", 0, 2)
-        h2_out("S", 0, 3)
+        make_larger(1, LAST_TILE)
+        make_z(1)
+        u = [sb("u%d" % t, S, F32) for t in range(PACK)]
+        for t in range(PACK):
+            scalar_empties(u[t][:, half(0)], h2_bank[(0, t)], 0.5)
         second_product(1)
-        h2_out("V", 1, 0)
-        h2_out("S", 1, 1)
-        h2_out("V", 1, 2)
-        look3("S", 0, 0)
-        look3("V", 0, 1)
-        look3("S", 1, 1)
-        look3("V", 1, 0)
-        h2_out("S", 1, 3)
-        look3("S", 3, 0)
-        look3("S", 3, 1)
-        look3("S", 2, 0)
-        look3("S", 2, 1)
-        max3(0)
-        max3(1)
-        fused4(0, 0)
-        fused4(0, 1)
-        look4(1, 0)
-        look4(1, 1)
-        max3(3)
-        max3(2)
-        look4(1, 3)
-        look4(1, 2)
-        sub4(1, 0)
-        fused4(0, 2)
-        fused4(0, 3)
-        store_out(0)
-        weave_o("S", 0)
-        sub4(1, 1)
-        sub4(1, 3)
-        sub4(1, 2)
-        store_out(1)
-        weave_o("V", 1)
-        planes_out(0)
-        planes_out(1)
-        scales_out()
+
+        h2_n3 = [sb("h2_n3_%d" % t, S, F32) for t in range(PACK)]
+        st2 = [sb("st2_%d" % t, S, F32) for t in range(PACK)]
+        st2_n4 = [sb("st2_n4_%d" % t, HALF, F32) for t in range(PACK)]
+        result = [sb("result%d" % a, PACK * HALF, F32) for a in range(2)]
+        result_woven = [sb("result_woven%d" % a, PACK * HALF, BF16) for a in range(2)]
+        out_words = sb("out_words", S, U32)
+        out_plane = sb("out_plane", S, U8)
+
+        def scalar_n3(t, a):
+            nc.scalar.activation(h2_n3[t][:, half(a)], u[t][:].indirect(half_entries(n3_list, a)), COPY, scale=2.0)
+
+        def vector_n3(t, a):
+            nc.vector.tensor_scalar(h2_n3[t][:, half(a)], u[t][:].indirect(half_entries(n3_list, a)), 2.0, 0.0, MULT, ADD)
+
+        def make_st2(t):
+            nc.vector.scalar_tensor_tensor(st2[t][:], u[t][:], 2.0, h2_n3[t][:], MULT, MAX)
+
+        def first_half_result(t):
+            nc.vector.tensor_tensor(result[0][:, slot(t)], st2[t][:].indirect(half_entries(n4_list, 0)), u[t][:, half(0)], SUB)
+
+        def second_half_look_up(t):
+            scalar_gather(st2_n4[t][:], st2[t], half_entries(n4_list, 1))
+
+        def second_half_result(t):
+            nc.vector.tensor_tensor(result[1][:, slot(t)], st2_n4[t][:], u[t][:, half(1)], SUB)
+
+        def store_result(a):
+            rows = out_0.rearrange("(p t) j -> p t j", t=PACK)
+            nc.sync.dma_start(out=rows[:, :, half(a)], in_=result[a][:].rearrange("p (t j) -> p t j", t=PACK))
+
+        def quantise_result(a):
+            nc.vector.quantize_mx(out=out_words[:, half(a)].bitcast(FP8X4), scales=out_plane[:, half(a)], in_=result_woven[a][:])
+            words = out_1[0].rearrange("p n t -> p (n t)").bitcast(I32)
+            nc.sync.dma_start(out=words[:, half(a)], in_=out_words[:, half(a)].bitcast(I32))
+
+        vector_empties(u[0][:, half(1)], h2_bank[(1, 0)], 0.5)
+        scalar_empties(u[1][:, half(1)], h2_bank[(1, 1)], 0.5)
+        vector_empties(u[2][:, half(1)], h2_bank[(1, 2)], 0.5)
+        for t in (0, 1):
+            scalar_n3(t, t)
+            vector_n3(t, 1 - t)
+        scalar_empties(u[3][:, half(1)], h2_bank[(1, 3)], 0.5)
+        for t in (3, 2):
+            for a in range(2):
+                scalar_n3(t, a)
+        for step in (make_st2, first_half_result, second_half_look_up):
+            for t in (0, 1):
+                step(t)
+        for step in (make_st2, second_half_look_up):
+            for t in (3, 2):
+                step(t)
+        second_half_result(0)
+        for t in (2, 3):
+            first_half_result(t)
+        store_result(0)
+        nc.scalar.copy(woven(result_woven[0]), side_by_side(result[0]))
+        for t in (1, 3, 2):
+            second_half_result(t)
+        store_result(1)
+        nc.vector.tensor_copy(woven(result_woven[1]), side_by_side(result[1]))
+        for a in range(2):
+            quantise_result(a)
+        for q in range(4):
+            engine = nc.scalar if q % 2 else nc.sync
+            engine.dma_start(out=out_2[0, 4 * q : 4 * q + 4, :].bitcast(I32), in_=out_plane[32 * q : 32 * q + 4, :].bitcast(I32))

from contextlib import ExitStack

import concourse.mybir as mybir

F32 = mybir.dt.float32
BF16 = mybir.dt.bfloat16
I32 = mybir.dt.int32
U32 = mybir.dt.uint32
U16 = mybir.dt.uint16
U8 = mybir.dt.uint8
FP8X4 = mybir.dt.float8_e4m3fn_x4
FP4X4 = mybir.dt.float4_e2m1fn_x4
COPY = mybir.ActivationFunctionType.Copy
ADD = mybir.AluOpType.add
MAX = mybir.AluOpType.max
MULT = mybir.AluOpType.mult
SUB = mybir.AluOpType.subtract

P = 128
PACK = 4
S = 512
TOKENS = 1024
CODEWORDS = 2048
BLOCKS = 16
HALF = S // 2
GROUP = 16
LINE = 4
SPARE = 16
VECTOR_TILE = 3
LAST_TILE = 2
EARLY_TILES = (3, 0, 1)
FLOPS = 3 * 2 * 512 * 512 * 512


def tile_picked_pqmixghopmhopb_none_po_kernel(
    tc, x_words, x_scales, d_words, d_scales, gn, w1_words, w1_scales, w2_words, w2_scales,
    offs, k1, n1, n2, two, n3, n4, out_0, out_1, out_2,
):
    nc = tc.nc
    with ExitStack() as ctx:
        keep = ctx.enter_context(tc.tile_pool(name="keep", bufs=1))
        reused = ctx.enter_context(tc.tile_pool(name="reused", bufs=1))
        psum = ctx.enter_context(tc.psum_pool(name="psum", bufs=8))

        def sb(name, width, dtype):
            return keep.tile([P, width], dtype, name=name, align_bytes=64)

        def placed(name, width, dtype, offset):
            return reused.tile([P, width], dtype, name=name, offset=offset, align_bytes=64)

        def half(a):
            return slice(HALF * a, HALF * (a + 1))

        def slot(t):
            return slice(HALF * t, HALF * (t + 1))

        def half_entries(list_tile, a):
            return list_tile[:, HALF // GROUP * a : HALF // GROUP * (a + 1)]

        def load_list(name, src):
            list_tile = keep.tile([P, src.shape[1]], U16, name=name)
            nc.sync.dma_start(list_tile[:], src)
            return list_tile

        def load_words(engine, tile, src):
            engine.dma_start(out=tile[:].bitcast(I32), in_=src.bitcast(I32))

        def load_scale_rows(engine, tile, scales):
            rows = scales[0].bitcast(I32)
            engine.dma_start(out=tile[:].bitcast(I32), in_=rows.unsqueeze(1).to_broadcast([BLOCKS, P // BLOCKS, rows.shape[1]]))

        def rows_to_plane(engine, plane, rows):
            for q in range(4):
                engine.dma_start(out=plane[32 * q : 32 * q + 4, :].bitcast(I32), in_=rows[32 * q : 32 * q + 32 : 8, :].bitcast(I32))

        def deal_bytes(engine, dst, src):
            engine.tensor_copy(dst.rearrange("p (t m) -> p t m", t=PACK), src.rearrange("p (m t) -> p t m", t=PACK))

        def woven(tile):
            return tile[:].rearrange("p (c i t) -> p c t i", i=LINE, t=PACK)

        def side_by_side(tile):
            return tile[:].rearrange("p (t c i) -> p c t i", i=LINE, t=PACK)

        def vector_gather(out, window, offsets):
            nc.vector.tensor_copy(out, window[:].indirect(offsets))

        def scalar_gather(out, window, offsets):
            nc.scalar.activation(out, window[:].indirect(offsets), COPY)

        def vector_empties(out, bank, factor):
            nc.vector.tensor_scalar(out, bank[:], factor, None, MULT)

        def scalar_empties(out, bank, factor):
            nc.scalar.activation(out, bank[:], COPY, scale=factor)

        d_rows = sb("d_rows", CODEWORDS, U8)
        x_rows = sb("x_rows", TOKENS, U8)
        x_table = sb("x_table", TOKENS, U32)
        d_table = sb("d_table", CODEWORDS, U32)
        k1_list = load_list("k1_list", k1)
        load_scale_rows(nc.sync, d_rows, d_scales)
        offs_list = load_list("offs_list", offs)
        load_scale_rows(nc.sync, x_rows, x_scales)
        load_words(nc.sync, x_table, x_words[0].rearrange("p n t -> p (n t)"))
        load_words(nc.sync, d_table, d_words[0].rearrange("p n t -> p (n t)"))
        two_list = load_list("two_list", two)
        n1_list = load_list("n1_list", n1)
        n2_list = load_list("n2_list", n2)
        n3_list = load_list("n3_list", n3)
        n4_list = load_list("n4_list", n4)

        w_words = [sb("w1_words", 2 * S, U8), sb("w2_words", 2 * S, U8)]
        w_rows = [sb("w1_rows", S, U8), sb("w2_rows", S, U8)]
        load_words(nc.gpsimd, w_words[0], w1_words[0])
        load_words(nc.gpsimd, w_words[1], w2_words[0])
        load_scale_rows(nc.gpsimd, w_rows[0], w1_scales)
        load_scale_rows(nc.gpsimd, w_rows[1], w2_scales)
        gain = sb("gain", PACK, F32)
        nc.gpsimd.dma_start(out=gain[:], in_=gn.rearrange("(p t) o -> p (t o)", t=PACK))

        first_plane = sb("first_plane", 2 * S, U8)
        two_plane = sb("two_plane", S, U8)
        w_plane = sb("w_plane", 2 * S, U8)
        for plane in (first_plane, two_plane, w_plane):
            nc.vector.memset(plane[:].bitcast(I32), 0)
        h = [sb("h%d" % t, (S if t == VECTOR_TILE else 2 * S) + SPARE, F32) for t in range(PACK)]
        st = [sb("st%d" % t, S + SPARE, F32) for t in range(PACK)]
        for t in range(PACK):
            nc.vector.memset(h[t][:, S:], 0.0)
            nc.vector.memset(st[t][:, S:], 0.0)

        picked_rows = placed("picked_rows", 2 * S, U8, 16 * S)
        first_rows = placed("first_rows", 2 * S, U8, 3 * S)
        dk_words = placed("dk_words", S, U32, 6 * S)
        vector_gather(picked_rows[:, :S], d_rows, k1_list[:])
        vector_gather(picked_rows[:, S:], x_rows, offs_list[:])
        deal_bytes(nc.vector, first_rows[:, :S], picked_rows[:, :S])
        nc.vector.tensor_copy(first_rows[:, S:].bitcast(I32), picked_rows[:, S:].bitcast(I32))
        rows_to_plane(nc.scalar, first_plane, first_rows)
        xq_words = placed("xq_words", S, U32, 16 * S)
        vector_gather(xq_words[:], x_table, offs_list[:])
        vector_gather(dk_words[:], d_table, k1_list[:])
        dk_dealt = sb("dk_dealt", S, U32)
        nc.vector.tensor_copy(side_by_side(dk_dealt), woven(dk_words))

        w_words_dealt = placed("w_words_dealt", 4 * S, U8, 0)
        w_rows_dealt = placed("w_rows_dealt", 2 * S, U8, 4 * S)
        for i in range(2):
            deal_bytes(nc.gpsimd, w_rows_dealt[:, S * i : S * (i + 1)], w_rows[i][:])
        rows_to_plane(nc.sync, w_plane, w_rows_dealt)
        for i in range(2):
            nc.gpsimd.tensor_copy(
                w_words_dealt[:, 2 * S * i : 2 * S * (i + 1)].rearrange("p (t m b) -> p t m b", t=PACK, b=2),
                w_words[i][:].rearrange("p (m t b) -> p t m b", t=PACK, b=2),
            )

        h_bank = {}
        for t in (0, 1, VECTOR_TILE, LAST_TILE):
            h_bank[t] = psum.tile([P, S], F32, name="bank")
            nc.tensor.matmul_mx(
                out=h_bank[t][:], lhsT=dk_dealt[:, P * t : P * (t + 1)].bitcast(FP8X4), lhsT_scale=first_plane[:, P * t : P * (t + 1)],
                rhs=xq_words[:].bitcast(FP8X4), rhs_scale=first_plane[:, S:], start=True, stop=True,
            )

        mb = [sb("mb%d" % t, 2 * S, F32) for t in range(PACK)]
        scalar_empties(h[0][:, :S], h_bank[0], 0.0625)
        scalar_empties(h[1][:, :S], h_bank[1], 0.0625)
        scalar_gather(mb[0][:], h[0], n1_list[:])

        two_rows = placed("two_rows", S, U8, 6 * S)
        two_words = placed("two_words", S, U32, 7 * S)
        vector_gather(two_rows[:], x_rows, two_list[:])
        rows_to_plane(nc.sync, two_plane, two_rows)
        vector_gather(two_words[:], x_table, two_list[:])

        vector_empties(h[VECTOR_TILE][:, :S], h_bank[VECTOR_TILE], 0.0625)
        vector_empties(h[LAST_TILE][:, :S], h_bank[LAST_TILE], 0.0625)
        scalar_gather(mb[1][:], h[1], n1_list[:])
        for a in range(2):
            vector_gather(mb[VECTOR_TILE][:, S * a : S * (a + 1)], h[VECTOR_TILE], n1_list[:, S // GROUP * a : S // GROUP * (a + 1)])
        scalar_gather(mb[LAST_TILE][:], h[LAST_TILE], n1_list[:])

        mx = [placed("mx_last", S, F32, 12 * S) if t == LAST_TILE else sb("mx%d" % t, S, F32) for t in range(PACK)]
        on_mx_last = {(1, 0): 12 * S, (1, 1): 14 * S}
        st_n2 = {
            (a, t): placed("st_n2_%d%d" % (a, t), HALF, F32, on_mx_last[(a, t)]) if (a, t) in on_mx_last else sb("st_n2_%d%d" % (a, t), HALF, F32)
            for a in range(2)
            for t in range(PACK)
        }
        larger = [sb("larger%d" % a, PACK * HALF, F32) for a in range(2)]
        z_woven = [sb("z_woven%d" % a, PACK * HALF, BF16) for a in range(2)]
        h2_bank = {}

        def larger_member(t):
            nc.vector.tensor_tensor(mx[t][:], mb[t][:, 0 : 2 * S : 2], mb[t][:, 1 : 2 * S : 2], MAX)

        def make_st(t):
            nc.vector.tensor_tensor(st[t][:, :S], h[t][:, :S], mx[t][:], SUB)

        def look_up_n2(a, t):
            scalar_gather(st_n2[(a, t)][:], st[t], half_entries(n2_list, a))

        def make_larger(a, t):
            nc.vector.tensor_tensor(larger[a][:, slot(t)], st[t][:, half(a)], st_n2[(a, t)][:], MAX)

        def make_z(a):
            spread = gain[:].unsqueeze(1).unsqueeze(3).to_broadcast([P, HALF // LINE, PACK, LINE])
            nc.vector.tensor_tensor(woven(z_woven[a]), side_by_side(larger[a]), spread, MULT)

        def second_product(a):
            z_words = sb("z_words%d" % a, HALF, U32)
            z_plane = sb("z_plane%d" % a, HALF, U8)
            nc.vector.quantize_mx(out=z_words[:].bitcast(FP8X4), scales=z_plane[:], in_=z_woven[a][:])
            for t in range(PACK):
                h2_bank[(a, t)] = psum.tile([P, HALF], F32, name="bank")
                operands = ((1, two_words[:, half(a)], two_plane[:, half(a)]), (0, z_words[:], z_plane[:]))
                for i, words, plane in operands:
                    first = S * i + P * t
                    nc.tensor.matmul_mx(
                        out=h2_bank[(a, t)][:], lhsT=w_words_dealt[:, 2 * first : 2 * (first + P)].bitcast(FP4X4),
                        lhsT_scale=w_plane[:, first : first + P], rhs=words.bitcast(FP8X4), rhs_scale=plane,
                        start=(i == 1), stop=(i == 0),
                    )

        for t in (0, VECTOR_TILE, 1):
            larger_member(t)
        for t in EARLY_TILES:
            make_st(t)
        larger_member(LAST_TILE)
        for t in EARLY_TILES:
            look_up_n2(0, t)
        make_st(LAST_TILE)
        look_up_n2(0, LAST_TILE)
        for t in EARLY_TILES + (LAST_TILE,):
            look_up_n2(1, t)
        for t in EARLY_TILES + (LAST_TILE,):
            make_larger(0, t)
        make_larger(1, EARLY_TILES[0])
        make_z(0)
        for t in EARLY_TILES[1:]:
            make_larger(1, t)
        second_product(0)
        make_larger(1, LAST_TILE)
        make_z(1)
        u = [sb("u%d" % t, S, F32) for t in range(PACK)]
        for t in range(PACK):
            scalar_empties(u[t][:, half(0)], h2_bank[(0, t)], 0.5)
        second_product(1)

        h2_n3 = [sb("h2_n3_%d" % t, S, F32) for t in range(PACK)]
        st2 = [sb("st2_%d" % t, S, F32) for t in range(PACK)]
        st2_n4 = [sb("st2_n4_%d" % t, HALF, F32) for t in range(PACK)]
        result = [sb("result%d" % a, PACK * HALF, F32) for a in range(2)]
        result_woven = [sb("result_woven%d" % a, PACK * HALF, BF16) for a in range(2)]
        out_words = sb("out_words", S, U32)
        out_plane = sb("out_plane", S, U8)

        def scalar_n3(t, a):
            nc.scalar.activation(h2_n3[t][:, half(a)], u[t][:].indirect(half_entries(n3_list, a)), COPY, scale=2.0)

        def vector_n3(t, a):
            nc.vector.tensor_scalar(h2_n3[t][:, half(a)], u[t][:].indirect(half_entries(n3_list, a)), 2.0, 0.0, MULT, ADD)

        def make_st2(t):
            nc.vector.scalar_tensor_tensor(st2[t][:], u[t][:], 2.0, h2_n3[t][:], MULT, MAX)

        def first_half_result(t):
            nc.vector.tensor_tensor(result[0][:, slot(t)], st2[t][:].indirect(half_entries(n4_list, 0)), u[t][:, half(0)], SUB)

        def second_half_look_up(t):
            scalar_gather(st2_n4[t][:], st2[t], half_entries(n4_list, 1))

        def second_half_result(t):
            nc.vector.tensor_tensor(result[1][:, slot(t)], st2_n4[t][:], u[t][:, half(1)], SUB)

        def store_result(a):
            rows = out_0.rearrange("(p t) j -> p t j", t=PACK)
            nc.sync.dma_start(out=rows[:, :, half(a)], in_=result[a][:].rearrange("p (t j) -> p t j", t=PACK))

        def quantise_result(a):
            nc.vector.quantize_mx(out=out_words[:, half(a)].bitcast(FP8X4), scales=out_plane[:, half(a)], in_=result_woven[a][:])
            words = out_1[0].rearrange("p n t -> p (n t)").bitcast(I32)
            nc.sync.dma_start(out=words[:, half(a)], in_=out_words[:, half(a)].bitcast(I32))

        vector_empties(u[0][:, half(1)], h2_bank[(1, 0)], 0.5)
        scalar_empties(u[1][:, half(1)], h2_bank[(1, 1)], 0.5)
        vector_empties(u[2][:, half(1)], h2_bank[(1, 2)], 0.5)
        for t in (0, 1):
            scalar_n3(t, t)
            vector_n3(t, 1 - t)
        scalar_empties(u[3][:, half(1)], h2_bank[(1, 3)], 0.5)
        for t in (3, 2):
            for a in range(2):
                scalar_n3(t, a)
        for step in (make_st2, first_half_result, second_half_look_up):
            for t in (0, 1):
                step(t)
        for step in (make_st2, second_half_look_up):
            for t in (3, 2):
                step(t)
        second_half_result(0)
        for t in (2, 3):
            first_half_result(t)
        store_result(0)
        nc.scalar.copy(woven(result_woven[0]), side_by_side(result[0]))
        for t in (1, 3, 2):
            second_half_result(t)
        store_result(1)
        nc.vector.tensor_copy(woven(result_woven[1]), side_by_side(result[1]))
        for a in range(2):
            quantise_result(a)
        for q in range(4):
            engine = nc.scalar if q % 2 else nc.sync
            engine.dma_start(out=out_2[0, 4 * q : 4 * q + 4, :].bitcast(I32), in_=out_plane[32 * q : 32 * q + 4, :].bitcast(I32))
